import numpy as np
import ml_dtypes


def mxq(x, axis, fmt="e4m3"):
    dtype, down = {"e4m3": (ml_dtypes.float8_e4m3fn, 7), "e5m2": (ml_dtypes.float8_e5m2, 14)}[fmt]
    v = np.moveaxis(np.asarray(x, np.float32).astype(ml_dtypes.bfloat16).astype(np.float64), axis, -1)
    blocks = v.reshape(v.shape[:-1] + (-1, 32))
    amax = np.abs(blocks).max(-1, keepdims=True)
    byte = np.maximum(np.where(amax > 0, np.frexp(amax)[1] - 1 + 127, 0) - down, 1)
    scale = np.exp2(byte - 127.0)
    codes = (blocks / scale).astype(np.float32).astype(dtype).astype(np.float64)
    return np.moveaxis((codes * scale).reshape(v.shape), -1, axis)


WIDE = False


def mx_kscale(k):
    if not WIDE:
        return np.ones(k)
    levels = np.array([10, -10, 5, -5, 0])
    if k % 512:
        return np.exp2(np.random.permutation(np.resize(levels, k // 32))).repeat(32)
    a = np.empty((k // 512, 16))
    for p in range(k // 512):
        a[p, :8] = np.random.permutation(np.resize(levels, 8))
        for g in range(8):
            far = levels[np.abs(levels - a[p, g]) >= 10]
            a[p, g + 8] = far[np.random.randint(len(far))]
    return np.exp2(a.ravel()).repeat(32)


def f64(x):
    return np.asarray(x).astype(np.float64)


def striped(idx):
    return np.tile(idx.reshape(-1, 16).T, (8, 1)).astype(np.uint16)


def unstriped(offs):
    return offs[:16].T.reshape(-1).astype(np.int64)


E2M1 = np.array([0.0, 0.5, 1.0, 1.5, 2.0, 3.0, 4.0, 6.0, -0.0, -0.5, -1.0, -1.5, -2.0, -3.0, -4.0, -6.0])


def pack_weight(w, fmt):
    k, n = w.shape
    w = f64(np.asarray(w, np.float32).astype(ml_dtypes.bfloat16)).reshape(k // 32, 32, n)
    amax = np.abs(w).max(1)
    if fmt == "e4m3":
        byte = np.frexp(amax)[1] - 1 + 127 - 7
    else:
        mant, ex = np.frexp(amax / 6.0)
        byte = np.where(mant > 0.5, ex, ex - 1) + 127
    byte = np.clip(np.where(amax > 0, byte, 1), 1, 254)
    scaled = (w * np.exp2(127.0 - byte)[:, None, :]).reshape(k, n).astype(np.float32)
    by_word = np.ascontiguousarray(scaled.reshape(k // 512, 128, 4, n).transpose(0, 1, 3, 2))
    if fmt == "e4m3":
        words = by_word.astype(ml_dtypes.float8_e4m3fn).view(np.uint8)
    else:
        c = by_word.astype(ml_dtypes.float4_e2m1fn).view(np.uint8) & 0xF
        words = (c[..., 0::2] | (c[..., 1::2] << 4)).reshape(k // 512, 128, 2 * n)
    return np.ascontiguousarray(words), np.ascontiguousarray(byte.astype(np.uint8).reshape(k // 512, 16, n))


def unpack_weight(words, scales, fmt):
    g, _, n = scales.shape
    words = np.ascontiguousarray(words).reshape(g, 128, n, -1)
    if fmt == "e4m3":
        vals = words.view(ml_dtypes.float8_e4m3fn).astype(np.float64)
    else:
        nib = np.empty((g, 128, n, 4), np.uint8)
        nib[..., 0::2] = words & 0xF
        nib[..., 1::2] = words >> 4
        vals = E2M1[nib]
    vals = vals * np.repeat(np.exp2(scales.astype(np.float64) - 127.0), 8, axis=1)[..., None]
    return vals.transpose(0, 1, 3, 2).reshape(g * 512, n)


def gelu(v):
    return 0.5 * v * (1.0 + np.tanh(np.sqrt(2.0 / np.pi) * (v + 0.044715 * v**3)))


K, H, T, S, P, P2 = 512, 1024, 4096, 2048, 1024, 512

def setup_inputs():
    n = np.random.standard_normal
    s = mx_kscale(K)[:, None]
    u = mx_kscale(H)[:, None]
    tab_words, tab_scales = pack_weight(n((K, T)) * s, "e4m3")
    w2_words, w2_scales = pack_weight(2.0 * n((H, H)) / np.sqrt(H) / u, "e2m1")
    return {
        "tab_words": tab_words, "tab_scales": tab_scales,
        "offs": striped(np.random.permutation(T)[:S]),
        "pos1": striped(np.random.permutation(S)[:P]),
        "pos2": striped(np.random.permutation(S)[:P]),
        "pos3": striped(np.random.permutation(P)[:P2]),
        "pos4": striped(np.random.permutation(S)[:P2]),
        "w1": (1.5 * n((K, H)) / np.sqrt(K) / s).astype(np.float32),
        "gain": (np.exp(0.3 * n(H)) * u[:, 0]).astype(np.float32),
        "w2_words": w2_words, "w2_scales": w2_scales,
        "w3": (1.2 * n((H, H)) / np.sqrt(H) / u).astype(np.float32),
    }

def reference(tab_words, tab_scales, offs, pos1, pos2, pos3, pos4, w1, gain, w2_words, w2_scales, w3):
    v = unpack_weight(tab_words, tab_scales, "e4m3")[:, unstriped(offs)]
    h = np.tanh(mxq(f64(w1), 0, "e4m3").T @ v)
    a1 = h[:, unstriped(pos1)] * h[:, unstriped(pos2)]
    a2 = np.maximum(a1[:, unstriped(pos3)], h[:, unstriped(pos4)])
    x = mxq(f64(gain)[:, None] * a2, 0, "e4m3")
    y1 = unpack_weight(w2_words, w2_scales, "e2m1").T @ x
    y2 = mxq(f64(w3), 0, "e4m3").T @ x
    return y1 / (1.0 + np.exp(-y1)) + y2 + a2

@@ -1,0 +1,356 @@
+from contextlib import ExitStack
+
+import concourse.mybir as mybir
+from concourse.masks import make_identity
+
+K, H, T, S, PAIRS, KEPT = 512, 1024, 4096, 2048, 1024, 512
+FLOPS = 2 * K * H * S + 2 * 2 * H * H * KEPT
+
+F32 = mybir.dt.float32
+BF16 = mybir.dt.bfloat16
+I32 = mybir.dt.int32
+U32 = mybir.dt.uint32
+U16 = mybir.dt.uint16
+U8 = mybir.dt.uint8
+FP8X4 = mybir.dt.float8_e4m3fn_x4
+FP4X4 = mybir.dt.float4_e2m1fn_x4
+ACT = mybir.ActivationFunctionType
+ALU = mybir.AluOpType
+
+P = 128
+PACK = 4
+PASS = P * PACK
+BANK = 512
+CHUNK = 128
+NCHUNK = KEPT // CHUNK
+
+
+def tile_list_segment_triangulation_scores_kernel(
+    tc, tab_words, tab_scales, offs, pos1, pos2, pos3, pos4, w1, gain, w2_words, w2_scales, w3, out
+):
+    nc = tc.nc
+    with ExitStack() as ctx:
+        keep = ctx.enter_context(tc.tile_pool(name="keep", bufs=1))
+        ring = ctx.enter_context(tc.tile_pool(name="ring", bufs=2))
+        psum = ctx.enter_context(tc.psum_pool(name="psum", bufs=1))
+
+        offs_t = keep.tile([P, S // 16], U16, name="offs_t")
+        pos1_t = keep.tile([P, PAIRS // 16], U16, name="pos1_t")
+        pos2_t = keep.tile([P, PAIRS // 16], U16, name="pos2_t")
+        pos3_t = keep.tile([P, KEPT // 16], U16, name="pos3_t")
+        pos4_t = keep.tile([P, KEPT // 16], U16, name="pos4_t")
+
+        tab_s = keep.tile([P, T], U8, name="tab_s", tag="stage_a", align_bytes=64)
+        tab_w = keep.tile([P, T], U32, name="tab_w", tag="stage_c", align_bytes=64)
+        gain_t = keep.tile([P, 2, PACK], F32, name="gain_t")
+        ident = keep.tile([P, P], F32, name="ident")
+
+        nc.sync.dma_start(out=tab_s[P - 16 :, :].bitcast(I32), in_=tab_scales[0].bitcast(I32))
+        nc.sync.dma_start(offs_t[:], offs)
+        nc.vector.memset(tab_s[0 : P - 16, :].bitcast(I32), 0)
+        make_identity(nc, ident[:])
+
+        def load_raw(w, a, half, pieces, tag):
+            raw = keep.tile([P, PACK, BANK], F32, name="raw", tag=tag, align_bytes=64)
+            width = BANK // pieces
+            for i in range(pieces):
+                c0 = half * BANK + i * width
+                nc.sync.dma_start(
+                    out=raw[:, :, i * width : (i + 1) * width],
+                    in_=w[a * PASS : (a + 1) * PASS, c0 : c0 + width].rearrange("(p j) c -> p j c", j=PACK),
+                )
+            return raw
+
+        def quantise(grouped, width, name):
+            codes = keep.tile([P, width], U32, name=name + "_c", align_bytes=64)
+            scales = keep.tile([P, width], U8, name=name + "_s", align_bytes=64)
+            nc.vector.quantize_mx(out=codes[:].bitcast(FP8X4), scales=scales[:], in_=grouped)
+            return codes, scales
+
+        def prepare_w1(raw, b, t0):
+            grouped = ring.tile([P, PACK * BANK], BF16, name="grouped", tag="grouped", align_bytes=64)
+            dst = grouped[:].rearrange("p (t m j) -> p m j t", t=PACK, j=PACK)
+            src = raw[:].rearrange("p j (m t) -> p m j t", t=PACK)
+            for m0 in (0, P // 2):
+                nc.scalar.copy(out=dst[:, m0 : m0 + P // 2, :, t0:], in_=src[:, m0 : m0 + P // 2, :, t0:])
+            codes, scales = quantise(grouped[:, t0 * BANK :], (PACK - t0) * P, "w1q%d" % b)
+            for t in range(t0, PACK):
+                cols = slice((t - t0) * P, (t - t0 + 1) * P)
+                w1_q[PACK * b + t] = (codes[:, cols], scales[:, cols])
+
+        def round_w3(raw):
+            grouped = ring.tile([P, PACK * BANK], BF16, name="grouped", tag="grouped", align_bytes=64)
+            nc.scalar.copy(
+                out=grouped[:].rearrange("p (c i j) -> p c j i", i=4, j=PACK),
+                in_=raw[:].rearrange("p j (c i) -> p c j i", i=4),
+            )
+            return grouped
+
+        nc.sync.dma_start(
+            out=tab_w[:].bitcast(I32), in_=tab_words[0].rearrange("p t i -> p (t i)").bitcast(I32)
+        )
+        nc.sync.dma_start(pos1_t[:], pos1)
+        nc.sync.dma_start(pos2_t[:], pos2)
+        nc.sync.dma_start(out=gain_t[:], in_=gain.rearrange("(b p t) -> p b t", b=2, t=PACK))
+        w1_raw0 = load_raw(w1, 0, 0, 2, "stage_b")
+        nc.sync.dma_start(pos4_t[:], pos4)
+        nc.sync.dma_start(pos3_t[:], pos3)
+
+        v_rows = keep.tile([P, S], U8, name="v_rows", tag="stage_d", align_bytes=64)
+        v_s = keep.tile([P, S], U8, name="v_s", align_bytes=64)
+        nc.vector.memset(v_s[:].bitcast(I32), 0)
+        nc.vector.tensor_copy(v_rows[:], tab_s[:].indirect(offs_t[:]))
+        for q in range(4):
+            nc.scalar.dma_start(
+                out=v_s[32 * q : 32 * q + 4, :].bitcast(I32),
+                in_=v_rows[P - 16 + 4 * q : P - 12 + 4 * q, :].bitcast(I32),
+            )
+        w1_raw1 = load_raw(w1, 0, 1, 1, "stage_a")
+        lead = keep.tile([P, PACK * P], BF16, name="lead", tag="v_w3", align_bytes=64)
+        for m0 in (0, P // 2):
+            nc.scalar.copy(
+                out=lead[:].rearrange("p (m j) -> p m j", j=PACK)[:, m0 : m0 + P // 2],
+                in_=w1_raw0[:].rearrange("p j (m t) -> p t m j", t=PACK)[:, 0, m0 : m0 + P // 2],
+            )
+        w1_q = {0: quantise(lead[:], P, "w1lead")}
+        v_w = []
+        for q in range(S // BANK):
+            piece = keep.tile([P, BANK], U32, name="v_w%d" % q, tag="v_w%d" % q, align_bytes=64)
+            nc.vector.tensor_copy(piece[:], tab_w[:].indirect(offs_t[:, 32 * q : 32 * q + 32]))
+            v_w.append(piece)
+
+        def features(s):
+            codes, scales = w1_q[s]
+            h = ring.tile([P, S], F32, name="h", tag="h", bufs=6)
+            for q in range(S // BANK):
+                acc = psum.tile([P, BANK], F32, name="acc", tag="acc", bufs=4)
+                nc.tensor.matmul_mx(
+                    out=acc[:],
+                    lhsT=codes[:].bitcast(FP8X4),
+                    lhsT_scale=scales[:],
+                    rhs=v_w[q][:].bitcast(FP8X4),
+                    rhs_scale=v_s[:, q * BANK : (q + 1) * BANK],
+                    start=True,
+                    stop=True,
+                )
+                nc.scalar.activation(out=h[:, q * BANK : (q + 1) * BANK], in_=acc[:], func=ACT.Tanh)
+            return h
+
+        hs = [features(0)]
+        prepare_w1(w1_raw0, 0, 1)
+        hs.extend(features(s) for s in range(1, 3))
+        prepare_w1(w1_raw1, 1, 0)
+        hs.extend(features(s) for s in range(3, 6))
+
+        w2_s = keep.tile([P, 2, H], U8, name="w2_s", tag="stage_d", align_bytes=64)
+        w2_w = keep.tile([P, 2, 2 * H], U8, name="w2_w", tag="stage_c", align_bytes=64)
+        nc.gpsimd.memset(w2_s[:].rearrange("p a c -> p (a c)").bitcast(I32), 0)
+        nc.sync.dma_start(
+            out=w2_w[:].bitcast(I32), in_=w2_words.rearrange("a p c -> p a c").bitcast(I32)
+        )
+        for q in range(4):
+            nc.sync.dma_start(
+                out=w2_s[32 * q : 32 * q + 4].bitcast(I32),
+                in_=w2_scales[:, 4 * q : 4 * q + 4, :].rearrange("a r c -> r a c").bitcast(I32),
+            )
+        w3_q = {}
+
+        def prepare_w3(a, half):
+            w3_q[(a, half)] = quantise(round_w3(load_raw(w3, a, half, 1, ("stage_b", "stage_a")[half]))[:], BANK, "w3q%d%d" % (a, half))
+
+        a2_lo = keep.tile([P, NCHUNK, PACK, CHUNK], F32, name="a2_lo")
+        a2_hi = [
+            keep.tile([P, PACK, CHUNK], F32, name="a2_hi%d" % c, tag="a2_hi%d" % c, align_bytes=64)
+            for c in range(NCHUNK)
+        ]
+        third_lo = keep.tile([P, PACK, KEPT // 2], F32, name="third_lo")
+        kept0 = keep.tile([P, PACK * CHUNK], F32, name="kept0")
+        xb_first = ring.tile([P, PACK, CHUNK], BF16, name="xb", tag="xb")
+        a1 = []
+        picked = {}
+        x_q0 = None
+
+        def pick_kept(dst, c, t):
+            nc.vector.tensor_copy(
+                dst[:, t * CHUNK : (t + 1) * CHUNK], a1[PACK + t][:].indirect(pos3_t[:, 8 * c : 8 * c + 8])
+            )
+
+        def scale_rows(xb, c, t):
+            nc.scalar.activation(
+                out=xb[:, t, :], in_=a2_hi[c][:, t, :], func=ACT.Copy, scale=gain_t[:, 1, t : t + 1]
+            )
+
+        def max_first(t):
+            nc.vector.tensor_tensor(
+                a2_hi[0][:, t, :], kept0[:, t * CHUNK : (t + 1) * CHUNK], third_lo[:, t, 0:CHUNK], ALU.max
+            )
+            scale_rows(xb_first, 0, t)
+
+        for s in range(2 * PACK):
+            b, t = divmod(s, PACK)
+            if s >= 1 and s + 5 < 2 * PACK:
+                hs.append(features(s + 5))
+            if 1 <= s <= 4:
+                prepare_w3(*divmod(s - 1, 2))
+            h = hs[s]
+            first = ring.tile([P, PAIRS], F32, name="first", tag="first")
+            nc.vector.tensor_copy(first[:], h[:].indirect(pos1_t[:]))
+            if 1 <= s <= PACK:
+                kept = ring.tile([P, KEPT], F32, name="kept", tag="kept")
+                nc.vector.tensor_copy(kept[:], a1[s - 1][:].indirect(pos3_t[:]))
+            elif s > PACK:
+                pick_kept(kept0, 0, t - 1)
+            if b == 0:
+                third = ring.tile([P, KEPT], F32, name="third", tag="third")
+                nc.vector.tensor_copy(third[:], h[:].indirect(pos4_t[:]))
+                picked[s] = third
+            else:
+                nc.vector.tensor_copy(third_lo[:, t, :], h[:].indirect(pos4_t[:, 0:16]))
+            if 1 <= s <= PACK:
+                nc.vector.tensor_tensor(
+                    a2_lo[:, :, s - 1, :],
+                    kept[:].rearrange("p (c j) -> p c j", c=NCHUNK),
+                    picked[s - 1][:].rearrange("p (c j) -> p c j", c=NCHUNK),
+                    ALU.max,
+                )
+            elif s > PACK:
+                max_first(t - 1)
+            pair = ring.tile([P, PAIRS], F32, name="pair", tag="pair", bufs=5)
+            nc.vector.tensor_tensor(pair[:], h[:].indirect(pos2_t[:]), first[:], ALU.mult)
+            a1.append(pair)
+            if s == PACK:
+                xb0 = keep.tile([P, PACK, KEPT], BF16, name="xb0")
+                for tt in range(PACK):
+                    nc.scalar.activation(
+                        out=xb0[:, tt, :].rearrange("p (c j) -> p c j", c=NCHUNK),
+                        in_=a2_lo[:, :, tt, :],
+                        func=ACT.Copy,
+                        scale=gain_t[:, 0, tt : tt + 1],
+                    )
+                xg0 = ring.tile([P, PACK * BANK], BF16, name="grouped", tag="grouped", align_bytes=64)
+                nc.scalar.copy(
+                    out=xg0[:].rearrange("p (c i t) -> p c t i", i=4, t=PACK),
+                    in_=xb0[:].rearrange("p t (c i) -> p c t i", i=4),
+                )
+            if s == PACK + 1:
+                x_q0 = quantise(xg0[:], KEPT, "xq0")
+
+        x_q1 = {}
+        xg = {}
+
+        def by_row(ap):
+            return ap.rearrange("p (t j) -> p t j", t=PACK)
+
+        def weave_scalar(c, xb, tag):
+            xg[c] = keep.tile([P, PACK * CHUNK], BF16, name="xg%d" % c, tag=tag, align_bytes=64)
+            nc.scalar.copy(
+                out=xg[c][:].rearrange("p (c i t) -> p c t i", i=4, t=PACK),
+                in_=xb[:].rearrange("p t (c i) -> p c t i", i=4),
+            )
+
+        def weave_vector(c, tag):
+            xg[c] = keep.tile([P, PACK * CHUNK], BF16, name="xg%d" % c, tag=tag, align_bytes=64)
+            nc.vector.tensor_tensor(
+                xg[c][:].rearrange("p (j t) -> p j t", t=PACK),
+                a2_hi[c][:].rearrange("p t j -> p j t"),
+                gain_t[:, 1:2, :].to_broadcast([P, CHUNK, PACK]),
+                ALU.mult,
+            )
+
+        def quantise_x(c):
+            x_q1[c] = quantise(xg[c][:], CHUNK, "xq1%d" % c)
+
+        summed = {}
+
+        def products(c):
+            cols = slice(c * CHUNK, (c + 1) * CHUNK)
+            x_ops = [
+                (x_q0[0][:, cols], x_q0[1][:, cols]),
+                (x_q1[c][0][:], x_q1[c][1][:]),
+            ]
+            for half in range(2):
+                y1 = psum.tile([P, BANK], F32, name="acc", tag="acc", bufs=4)
+                y2 = psum.tile([P, BANK], F32, name="acc", tag="acc", bufs=4)
+                for a in range(2):
+                    codes, scales = x_ops[a]
+                    nc.tensor.matmul_mx(
+                        out=y1[:],
+                        lhsT=codes.bitcast(FP8X4),
+                        lhsT_scale=scales,
+                        rhs=w2_w[:, a, 2 * BANK * half : 2 * BANK * (half + 1)].bitcast(FP4X4),
+                        rhs_scale=w2_s[:, a, BANK * half : BANK * (half + 1)],
+                        start=(a == 0),
+                        stop=(a == 1),
+                    )
+                    nc.tensor.matmul_mx(
+                        out=y2[:],
+                        lhsT=codes.bitcast(FP8X4),
+                        lhsT_scale=scales,
+                        rhs=w3_q[(a, half)][0][:].bitcast(FP8X4),
+                        rhs_scale=w3_q[(a, half)][1][:],
+                        start=(a == 0),
+                        stop=(a == 1),
+                    )
+                silu = ring.tile([P, PACK, P], F32, name="silu", tag="silu")
+                plain = ring.tile([P, PACK, P], F32, name="plain", tag="plain")
+                nc.scalar.activation(
+                    out=silu[:], in_=y1[:].rearrange("p (m t) -> p t m", t=PACK), func=ACT.Silu
+                )
+                nc.scalar.copy(out=plain[:], in_=y2[:].rearrange("p (m t) -> p t m", t=PACK))
+                turned = psum.tile([P, PACK, CHUNK], F32, name="turned", tag="turned", bufs=4)
+                for t in range(PACK):
+                    nc.tensor.matmul(turned[:, t, :], silu[:, t, :], ident[:], start=True, stop=False, is_transpose=True)
+                    nc.tensor.matmul(turned[:, t, :], plain[:, t, :], ident[:], start=False, stop=True, is_transpose=True)
+                summed[(c, half)] = turned
+
+        def finish(c):
+            cols = slice(c * CHUNK, (c + 1) * CHUNK)
+            for half in range(2):
+                result = ring.tile([P, PACK, CHUNK], F32, name="result", tag="result", bufs=3)
+                nc.vector.tensor_tensor(result[:], summed[(c, half)][:], (a2_lo[:, c], a2_hi[c][:])[half], ALU.add)
+                nc.sync.dma_start(
+                    out=out[half * PASS : (half + 1) * PASS, cols].rearrange("(p t) j -> p t j", t=PACK),
+                    in_=result[:],
+                )
+
+        kept1 = ring.tile([P, PAIRS], F32, name="first", tag="first")
+        pick_kept(kept1, 1, 0)
+        pick_kept(kept0, 0, 3)
+        pick_kept(kept1, 1, 1)
+        max_first(3)
+        weave_scalar(0, xb_first, "after_x0")
+        pick_kept(kept1, 1, 2)
+        pick_kept(kept1, 1, 3)
+        nc.vector.tensor_tensor(
+            a2_hi[1][:], by_row(kept1[:, 0 : PACK * CHUNK]), third_lo[:, :, CHUNK : 2 * CHUNK], ALU.max
+        )
+        xb_second = ring.tile([P, PACK, CHUNK], BF16, name="xb", tag="xb")
+        for t in range(PACK):
+            scale_rows(xb_second, 1, t)
+        weave_scalar(1, xb_second, "after_x1")
+        quantise_x(0)
+        products(0)
+        third_hi = keep.tile([P, PACK, KEPT // 2], F32, name="third_hi", tag="after_x0", align_bytes=64)
+        for t in range(PACK):
+            nc.vector.tensor_copy(third_hi[:, t, :], hs[PACK + t][:].indirect(pos4_t[:, 16:32]))
+        quantise_x(1)
+        products(1)
+        kept23 = keep.tile([P, 2, PACK * CHUNK], F32, name="kept23", tag="after_x1", align_bytes=64)
+        for t in range(PACK):
+            pick_kept(kept23[:, 0, :], 2, t)
+        pick_kept(kept23[:, 1, :], 3, 0)
+        nc.vector.tensor_tensor(a2_hi[2][:], by_row(kept23[:, 0, :]), third_hi[:, :, 0:CHUNK], ALU.max)
+        pick_kept(kept23[:, 1, :], 3, 1)
+        weave_vector(2, "xg2")
+        pick_kept(kept23[:, 1, :], 3, 2)
+        quantise_x(2)
+        pick_kept(kept23[:, 1, :], 3, 3)
+        finish(0)
+        nc.vector.tensor_tensor(a2_hi[3][:], by_row(kept23[:, 1, :]), third_hi[:, :, CHUNK : 2 * CHUNK], ALU.max)
+        products(2)
+        weave_vector(3, "a2_hi0")
+        finish(1)
+        quantise_x(3)
+        products(3)
+        finish(2)
+        finish(3)

@@ -49,40 +49,42 @@ def tile_list_segment_triangulation_scores_kernel(
         nc.sync.dma_start(offs_t[:], offs)
         nc.vector.memset(tab_s[0 : P - 16, :].bitcast(I32), 0)
         make_identity(nc, ident[:])
+        warm = keep.tile([P, 1], F32, name="warm")
+        nc.scalar.activation(out=warm[:], in_=ident[:, 0:1], func=ACT.Silu)
 
-        def load_raw(w, a, half, pieces, tag):
-            raw = keep.tile([P, PACK, BANK], F32, name="raw", tag=tag, align_bytes=64)
-            width = BANK // pieces
-            for i in range(pieces):
-                c0 = half * BANK + i * width
-                nc.sync.dma_start(
-                    out=raw[:, :, i * width : (i + 1) * width],
-                    in_=w[a * PASS : (a + 1) * PASS, c0 : c0 + width].rearrange("(p j) c -> p j c", j=PACK),
-                )
+        def load_raw(w, a, c0, width, tag):
+            raw = keep.tile([P, PACK, width], F32, name="raw", tag=tag, align_bytes=64)
+            nc.sync.dma_start(
+                out=raw[:],
+                in_=w[a * PASS : (a + 1) * PASS, c0 : c0 + width].rearrange("(p j) c -> p j c", j=PACK),
+            )
             return raw
 
-        def quantise(grouped, width, name):
-            codes = keep.tile([P, width], U32, name=name + "_c", align_bytes=64)
+        def quantise(grouped, width, name, tag=None):
+            codes = keep.tile([P, width], U32, name=name + "_c", tag=tag or name + "_c", align_bytes=64)
             scales = keep.tile([P, width], U8, name=name + "_s", align_bytes=64)
             nc.vector.quantize_mx(out=codes[:].bitcast(FP8X4), scales=scales[:], in_=grouped)
             return codes, scales
 
-        def prepare_w1(raw, b, t0):
+        def prepare_w1(raws, b, t0):
             grouped = ring.tile([P, PACK * BANK], BF16, name="grouped", tag="grouped", align_bytes=64)
             dst = grouped[:].rearrange("p (t m j) -> p m j t", t=PACK, j=PACK)
-            src = raw[:].rearrange("p j (m t) -> p m j t", t=PACK)
-            for m0 in (0, P // 2):
-                nc.scalar.copy(out=dst[:, m0 : m0 + P // 2, :, t0:], in_=src[:, m0 : m0 + P // 2, :, t0:])
+            for i, raw in enumerate(raws):
+                src = raw.rearrange("p j (m t) -> p m j t", t=PACK)
+                nc.scalar.copy(out=dst[:, i * P // 2 : (i + 1) * P // 2, :, t0:], in_=src[:, :, :, t0:])
             codes, scales = quantise(grouped[:, t0 * BANK :], (PACK - t0) * P, "w1q%d" % b)
             for t in range(t0, PACK):
                 cols = slice((t - t0) * P, (t - t0 + 1) * P)
                 w1_q[PACK * b + t] = (codes[:, cols], scales[:, cols])
 
-        def round_w3(raw):
-            grouped = ring.tile([P, PACK * BANK], BF16, name="grouped", tag="grouped", align_bytes=64)
+        def round_w3(raw, last):
+            if last:
+                grouped = keep.tile([P, PACK * BANK], BF16, name="grouped", tag="gate_b", align_bytes=64)
+            else:
+                grouped = ring.tile([P, PACK * BANK], BF16, name="grouped", tag="grouped", align_bytes=64)
             nc.scalar.copy(
-                out=grouped[:].rearrange("p (c i j) -> p c j i", i=4, j=PACK),
-                in_=raw[:].rearrange("p j (c i) -> p c j i", i=4),
+                out=grouped[:].rearrange("p (t m j) -> p m j t", t=PACK, j=PACK),
+                in_=raw[:].rearrange("p j (m t) -> p m j t", t=PACK),
             )
             return grouped
 
@@ -92,7 +94,7 @@ def tile_list_segment_triangulation_scores_kernel(
         nc.sync.dma_start(pos1_t[:], pos1)
         nc.sync.dma_start(pos2_t[:], pos2)
         nc.sync.dma_start(out=gain_t[:], in_=gain.rearrange("(b p t) -> p b t", b=2, t=PACK))
-        w1_raw0 = load_raw(w1, 0, 0, 2, "stage_b")
+        w1_raw0 = [load_raw(w1, 0, 0, BANK // 2, "stage_b")[:], load_raw(w1, 0, BANK // 2, BANK // 2, "stage_e")[:]]
         nc.sync.dma_start(pos4_t[:], pos4)
         nc.sync.dma_start(pos3_t[:], pos3)
 
@@ -101,16 +103,17 @@ def tile_list_segment_triangulation_scores_kernel(
         nc.vector.memset(v_s[:].bitcast(I32), 0)
         nc.vector.tensor_copy(v_rows[:], tab_s[:].indirect(offs_t[:]))
         for q in range(4):
-            nc.scalar.dma_start(
+            nc.sync.dma_start(
                 out=v_s[32 * q : 32 * q + 4, :].bitcast(I32),
                 in_=v_rows[P - 16 + 4 * q : P - 12 + 4 * q, :].bitcast(I32),
             )
-        w1_raw1 = load_raw(w1, 0, 1, 1, "stage_a")
+        w1_second = load_raw(w1, 0, BANK, BANK, "stage_a")
+        w1_raw1 = [w1_second[:, :, 0 : BANK // 2], w1_second[:, :, BANK // 2 :]]
         lead = keep.tile([P, PACK * P], BF16, name="lead", tag="v_w3", align_bytes=64)
-        for m0 in (0, P // 2):
+        for i, raw in enumerate(w1_raw0):
             nc.scalar.copy(
-                out=lead[:].rearrange("p (m j) -> p m j", j=PACK)[:, m0 : m0 + P // 2],
-                in_=w1_raw0[:].rearrange("p j (m t) -> p t m j", t=PACK)[:, 0, m0 : m0 + P // 2],
+                out=lead[:].rearrange("p (m j) -> p m j", j=PACK)[:, i * P // 2 : (i + 1) * P // 2],
+                in_=raw.rearrange("p j (m t) -> p t m j", t=PACK)[:, 0],
             )
         w1_q = {0: quantise(lead[:], P, "w1lead")}
         v_w = []
@@ -121,9 +124,15 @@ def tile_list_segment_triangulation_scores_kernel(
 
         def features(s):
             codes, scales = w1_q[s]
-            h = ring.tile([P, S], F32, name="h", tag="h", bufs=6)
+            if s < 2 * PACK - 1:
+                h = ring.tile([P, S], F32, name="h", tag="h", bufs=2 * PACK - 1)
+            else:
+                h = keep.tile([P, S], F32, name="h", tag="stage_c", align_bytes=64)
             for q in range(S // BANK):
-                acc = psum.tile([P, BANK], F32, name="acc", tag="acc", bufs=4)
+                if s < 2 * PACK - 1:
+                    acc = psum.tile([P, BANK], F32, name="acc", tag="acc", bufs=4)
+                else:
+                    acc = psum.tile([P, BANK], F32, name="acc", tag="turned%d" % q)
                 nc.tensor.matmul_mx(
                     out=acc[:],
                     lhsT=codes[:].bitcast(FP8X4),
@@ -140,11 +149,11 @@ def tile_list_segment_triangulation_scores_kernel(
         prepare_w1(w1_raw0, 0, 1)
         hs.extend(features(s) for s in range(1, 3))
         prepare_w1(w1_raw1, 1, 0)
-        hs.extend(features(s) for s in range(3, 6))
+        hs.extend(features(s) for s in range(3, 2 * PACK))
 
-        w2_s = keep.tile([P, 2, H], U8, name="w2_s", tag="stage_d", align_bytes=64)
-        w2_w = keep.tile([P, 2, 2 * H], U8, name="w2_w", tag="stage_c", align_bytes=64)
-        nc.gpsimd.memset(w2_s[:].rearrange("p a c -> p (a c)").bitcast(I32), 0)
+        w2_s = keep.tile([P, 2, H], U8, name="w2_s", tag="stage_e", align_bytes=64)
+        w2_w = keep.tile([P, 2, 2 * H], U8, name="w2_w", tag="stage_d", align_bytes=64)
+        nc.vector.memset(w2_s[:].rearrange("p a c -> p (a c)").bitcast(I32), 0)
         nc.sync.dma_start(
             out=w2_w[:].bitcast(I32), in_=w2_words.rearrange("a p c -> p a c").bitcast(I32)
         )
@@ -155,202 +164,302 @@ def tile_list_segment_triangulation_scores_kernel(
             )
         w3_q = {}
 
-        def prepare_w3(a, half):
-            w3_q[(a, half)] = quantise(round_w3(load_raw(w3, a, half, 1, ("stage_b", "stage_a")[half]))[:], BANK, "w3q%d%d" % (a, half))
+        w3_grouped = {}
+        for half in range(2):
+            for a in range(2):
+                raw = load_raw(w3, a, half * BANK, BANK, ("stage_b", "stage_a")[a])
+                w3_grouped[(a, half)] = round_w3(raw, (a, half) == (1, 0))
+                if half == 0:
+                    w3_q[(a, half)] = quantise(w3_grouped[(a, half)][:], BANK, "w3q%d0" % a)
 
-        a2_lo = keep.tile([P, NCHUNK, PACK, CHUNK], F32, name="a2_lo")
-        a2_hi = [
-            keep.tile([P, PACK, CHUNK], F32, name="a2_hi%d" % c, tag="a2_hi%d" % c, align_bytes=64)
-            for c in range(NCHUNK)
-        ]
-        third_lo = keep.tile([P, PACK, KEPT // 2], F32, name="third_lo")
-        kept0 = keep.tile([P, PACK * CHUNK], F32, name="kept0")
-        xb_first = ring.tile([P, PACK, CHUNK], BF16, name="xb", tag="xb")
+        HALF = KEPT // 2
+        a2_early = keep.tile([P, 2, PACK, CHUNK], F32, name="a2_early", tag="a2_early", align_bytes=64)
+        a2 = {(0, 0): a2_early[:, 0], (0, 1): a2_early[:, 1]}
+
+        def new_a2(key, tag):
+            a2[key] = keep.tile([P, PACK, CHUNK], F32, name="a2_%d%d" % key, tag=tag, align_bytes=64)[:]
+
+        for key in ((0, 2), (1, 0), (1, 1), (1, 2)):
+            new_a2(key, "a2_%d%d" % key)
+        third_lo = keep.tile([P, PACK, HALF], F32, name="third_lo")
+        kept0 = keep.tile([P, PACK * CHUNK], F32, name="kept0", tag="kept0", align_bytes=64)
+        xb_first = keep.tile([P, PACK, CHUNK], BF16, name="xb_first", tag="xb_first", align_bytes=64)
         a1 = []
         picked = {}
-        x_q0 = None
+        x_q = {}
+        xg = {}
 
-        def pick_kept(dst, c, t):
+        def pick_kept(dst, b, c, t):
             nc.vector.tensor_copy(
-                dst[:, t * CHUNK : (t + 1) * CHUNK], a1[PACK + t][:].indirect(pos3_t[:, 8 * c : 8 * c + 8])
+                dst[:, t * CHUNK : (t + 1) * CHUNK], a1[PACK * b + t][:].indirect(pos3_t[:, 8 * c : 8 * c + 8])
             )
+
+        def pick_third_hi(dst, b, t):
+            nc.vector.tensor_copy(dst[:, t * HALF : (t + 1) * HALF], hs[PACK * b + t][:].indirect(pos4_t[:, 16:32]))
 
         def scale_rows(xb, c, t):
             nc.scalar.activation(
-                out=xb[:, t, :], in_=a2_hi[c][:, t, :], func=ACT.Copy, scale=gain_t[:, 1, t : t + 1]
+                out=xb[:, t, :], in_=a2[(1, c)][:, t, :], func=ACT.Copy, scale=gain_t[:, 1, t : t + 1]
             )
 
         def max_first(t):
             nc.vector.tensor_tensor(
-                a2_hi[0][:, t, :], kept0[:, t * CHUNK : (t + 1) * CHUNK], third_lo[:, t, 0:CHUNK], ALU.max
+                a2[(1, 0)][:, t, :], kept0[:, t * CHUNK : (t + 1) * CHUNK], third_lo[:, t, 0:CHUNK], ALU.max
             )
             scale_rows(xb_first, 0, t)
 
+        a2_turned = {}
+
+        def turn_residual(b, c):
+            bank = psum.tile([P, PACK, P], F32, name="turned", tag="turned%d" % (2 + c))
+            for t in range(PACK):
+                nc.tensor.transpose(bank[:, t, :], a2[(b, c)][:, t, :], ident[:])
+            a2_turned[(b, c)] = keep.tile([P, PACK, P], F32, name="a2_turned%d%d" % (b, c))
+            nc.scalar.copy(out=a2_turned[(b, c)][:], in_=bank[:])
+
         for s in range(2 * PACK):
             b, t = divmod(s, PACK)
-            if s >= 1 and s + 5 < 2 * PACK:
-                hs.append(features(s + 5))
-            if 1 <= s <= 4:
-                prepare_w3(*divmod(s - 1, 2))
             h = hs[s]
-            first = ring.tile([P, PAIRS], F32, name="first", tag="first")
+            if s < 2 * PACK - 2:
+                first = ring.tile([P, PAIRS], F32, name="first", tag="first")
+            else:
+                first = keep.tile([P, PAIRS], F32, name="first", tag=("gate_b", "gate_a")[s % 2], align_bytes=64)
             nc.vector.tensor_copy(first[:], h[:].indirect(pos1_t[:]))
             if 1 <= s <= PACK:
-                kept = ring.tile([P, KEPT], F32, name="kept", tag="kept")
-                nc.vector.tensor_copy(kept[:], a1[s - 1][:].indirect(pos3_t[:]))
+                kept = ring.tile([P, HALF], F32, name="kept", tag="kept")
+                nc.vector.tensor_copy(kept[:], a1[s - 1][:].indirect(pos3_t[:, 0:16]))
             elif s > PACK:
-                pick_kept(kept0, 0, t - 1)
+                pick_kept(kept0, 1, 0, t - 1)
             if b == 0:
-                third = ring.tile([P, KEPT], F32, name="third", tag="third")
-                nc.vector.tensor_copy(third[:], h[:].indirect(pos4_t[:]))
+                third = ring.tile([P, HALF], F32, name="third", tag="third")
+                nc.vector.tensor_copy(third[:], h[:].indirect(pos4_t[:, 0:16]))
                 picked[s] = third
             else:
                 nc.vector.tensor_copy(third_lo[:, t, :], h[:].indirect(pos4_t[:, 0:16]))
+            pair = ring.tile([P, PAIRS], F32, name="pair", tag="pair", bufs=2 * PACK)
+            nc.vector.tensor_tensor(pair[:], h[:].indirect(pos2_t[:]), first[:], ALU.mult)
+            a1.append(pair)
             if 1 <= s <= PACK:
                 nc.vector.tensor_tensor(
-                    a2_lo[:, :, s - 1, :],
-                    kept[:].rearrange("p (c j) -> p c j", c=NCHUNK),
-                    picked[s - 1][:].rearrange("p (c j) -> p c j", c=NCHUNK),
+                    a2_early[:, :, s - 1, :],
+                    kept[:].rearrange("p (c j) -> p c j", c=2),
+                    picked[s - 1][:].rearrange("p (c j) -> p c j", c=2),
                     ALU.max,
                 )
             elif s > PACK:
                 max_first(t - 1)
-            pair = ring.tile([P, PAIRS], F32, name="pair", tag="pair", bufs=5)
-            nc.vector.tensor_tensor(pair[:], h[:].indirect(pos2_t[:]), first[:], ALU.mult)
-            a1.append(pair)
             if s == PACK:
-                xb0 = keep.tile([P, PACK, KEPT], BF16, name="xb0")
+                xb0 = keep.tile([P, PACK, HALF], BF16, name="xb0")
                 for tt in range(PACK):
                     nc.scalar.activation(
-                        out=xb0[:, tt, :].rearrange("p (c j) -> p c j", c=NCHUNK),
-                        in_=a2_lo[:, :, tt, :],
+                        out=xb0[:, tt, :].rearrange("p (c j) -> p c j", c=2),
+                        in_=a2_early[:, :, tt, :],
                         func=ACT.Copy,
                         scale=gain_t[:, 0, tt : tt + 1],
                     )
-                xg0 = ring.tile([P, PACK * BANK], BF16, name="grouped", tag="grouped", align_bytes=64)
+                xg0 = keep.tile([P, PACK * HALF], BF16, name="xg0", tag="gate_a", align_bytes=64)
                 nc.scalar.copy(
                     out=xg0[:].rearrange("p (c i t) -> p c t i", i=4, t=PACK),
                     in_=xb0[:].rearrange("p t (c i) -> p c t i", i=4),
                 )
+                turn_residual(0, 0)
+                turn_residual(0, 1)
             if s == PACK + 1:
-                x_q0 = quantise(xg0[:], KEPT, "xq0")
-
-        x_q1 = {}
-        xg = {}
+                codes, scales = quantise(xg0[:], HALF, "xq_early")
+                for c in range(2):
+                    cols = slice(c * CHUNK, (c + 1) * CHUNK)
+                    x_q[(0, c)] = (codes[:, cols], scales[:, cols])
 
         def by_row(ap):
             return ap.rearrange("p (t j) -> p t j", t=PACK)
 
         def weave_scalar(c, xb, tag):
-            xg[c] = keep.tile([P, PACK * CHUNK], BF16, name="xg%d" % c, tag=tag, align_bytes=64)
+            xg[(1, c)] = keep.tile([P, PACK * CHUNK], BF16, name="xg%d" % c, tag=tag, align_bytes=64)
             nc.scalar.copy(
-                out=xg[c][:].rearrange("p (c i t) -> p c t i", i=4, t=PACK),
+                out=xg[(1, c)][:].rearrange("p (c i t) -> p c t i", i=4, t=PACK),
                 in_=xb[:].rearrange("p t (c i) -> p c t i", i=4),
             )
 
-        def weave_vector(c, tag):
-            xg[c] = keep.tile([P, PACK * CHUNK], BF16, name="xg%d" % c, tag=tag, align_bytes=64)
+        def weave_vector(b, c, tag):
+            xg[(b, c)] = keep.tile([P, PACK * CHUNK], BF16, name="xv%d%d" % (b, c), tag=tag, align_bytes=64)
             nc.vector.tensor_tensor(
-                xg[c][:].rearrange("p (j t) -> p j t", t=PACK),
-                a2_hi[c][:].rearrange("p t j -> p j t"),
-                gain_t[:, 1:2, :].to_broadcast([P, CHUNK, PACK]),
+                xg[(b, c)][:].rearrange("p (c i t) -> p c t i", i=4, t=PACK),
+                a2[(b, c)].rearrange("p t (c i) -> p c t i", i=4),
+                gain_t[:, b : b + 1, :].unsqueeze(3).to_broadcast([P, CHUNK // 4, PACK, 4]),
                 ALU.mult,
             )
 
-        def quantise_x(c):
-            x_q1[c] = quantise(xg[c][:], CHUNK, "xq1%d" % c)
+        def quantise_x(b, c):
+            codes, scales = quantise(xg[(b, c)][:], CHUNK, "xq%d%d" % (b, c))
+            x_q[(b, c)] = (codes[:], scales[:])
+
+        def max_late(b, c, kept, third_hi):
+            nc.vector.tensor_tensor(
+                a2[(b, c)], by_row(kept), by_row(third_hi)[:, :, (c - 2) * CHUNK : (c - 1) * CHUNK], ALU.max
+            )
 
         summed = {}
 
+        def turned_product(bank, c, a, half, rhs, rhs_scale):
+            codes, scales = x_q[(a, c)]
+            nc.tensor.matmul_mx(
+                out=bank[:],
+                lhsT=codes.bitcast(FP8X4),
+                lhsT_scale=scales,
+                rhs=rhs,
+                rhs_scale=rhs_scale,
+                start=(a == 0),
+                stop=(a == 1),
+            )
+
+        def product_w2(bank, c, a, half):
+            turned_product(
+                bank,
+                c,
+                a,
+                half,
+                w2_w[:, a, 2 * BANK * half : 2 * BANK * (half + 1)].bitcast(FP4X4),
+                w2_s[:, a, BANK * half : BANK * (half + 1)],
+            )
+
+        def apply_silu(y1):
+            silu = ring.tile([P, PACK, P], F32, name="silu", tag="silu")
+            nc.scalar.activation(out=silu[:], in_=y1[:].rearrange("p (m t) -> p t m", t=PACK), func=ACT.Silu)
+            return silu
+
+        def turn_back(terms, c, half):
+            bank = ((0, 1), (2, 3), (0, 2), (1, 3))[c][half]
+            turned = psum.tile([P, PACK, CHUNK], F32, name="turned", tag="turned%d" % bank)
+            for t in range(PACK):
+                for i, term in enumerate(terms):
+                    nc.tensor.matmul(
+                        turned[:, t, :],
+                        term[:, t, :],
+                        ident[:],
+                        start=(i == 0),
+                        stop=(i == len(terms) - 1),
+                        is_transpose=True,
+                    )
+            return turned
+
+        def store(c, half, result):
+            nc.sync.dma_start(
+                out=out[half * PASS : (half + 1) * PASS, c * CHUNK : (c + 1) * CHUNK].rearrange(
+                    "(p t) j -> p t j", t=PACK
+                ),
+                in_=result[:],
+            )
+
         def products(c):
-            cols = slice(c * CHUNK, (c + 1) * CHUNK)
-            x_ops = [
-                (x_q0[0][:, cols], x_q0[1][:, cols]),
-                (x_q1[c][0][:], x_q1[c][1][:]),
-            ]
             for half in range(2):
                 y1 = psum.tile([P, BANK], F32, name="acc", tag="acc", bufs=4)
                 y2 = psum.tile([P, BANK], F32, name="acc", tag="acc", bufs=4)
                 for a in range(2):
-                    codes, scales = x_ops[a]
-                    nc.tensor.matmul_mx(
-                        out=y1[:],
-                        lhsT=codes.bitcast(FP8X4),
-                        lhsT_scale=scales,
-                        rhs=w2_w[:, a, 2 * BANK * half : 2 * BANK * (half + 1)].bitcast(FP4X4),
-                        rhs_scale=w2_s[:, a, BANK * half : BANK * (half + 1)],
-                        start=(a == 0),
-                        stop=(a == 1),
-                    )
-                    nc.tensor.matmul_mx(
-                        out=y2[:],
-                        lhsT=codes.bitcast(FP8X4),
-                        lhsT_scale=scales,
-                        rhs=w3_q[(a, half)][0][:].bitcast(FP8X4),
-                        rhs_scale=w3_q[(a, half)][1][:],
-                        start=(a == 0),
-                        stop=(a == 1),
-                    )
-                silu = ring.tile([P, PACK, P], F32, name="silu", tag="silu")
+                    product_w2(y1, c, a, half)
+                    turned_product(y2, c, a, half, w3_q[(a, half)][0][:].bitcast(FP8X4), w3_q[(a, half)][1][:])
+                silu = apply_silu(y1)
                 plain = ring.tile([P, PACK, P], F32, name="plain", tag="plain")
-                nc.scalar.activation(
-                    out=silu[:], in_=y1[:].rearrange("p (m t) -> p t m", t=PACK), func=ACT.Silu
-                )
-                nc.scalar.copy(out=plain[:], in_=y2[:].rearrange("p (m t) -> p t m", t=PACK))
-                turned = psum.tile([P, PACK, CHUNK], F32, name="turned", tag="turned", bufs=4)
-                for t in range(PACK):
-                    nc.tensor.matmul(turned[:, t, :], silu[:, t, :], ident[:], start=True, stop=False, is_transpose=True)
-                    nc.tensor.matmul(turned[:, t, :], plain[:, t, :], ident[:], start=False, stop=True, is_transpose=True)
-                summed[(c, half)] = turned
+                nc.scalar.copy(out=plain[:], in_=y2[:].rearrange("p (t m) -> p t m", t=PACK))
+                if (half, c) in a2_turned:
+                    turned = turn_back([silu, plain, a2_turned[(half, c)]], c, half)
+                    result = ring.tile([P, PACK, CHUNK], F32, name="result", tag="result", bufs=3)
+                    nc.scalar.copy(out=result[:], in_=turned[:])
+                    store(c, half, result)
+                else:
+                    summed[(c, half)] = turn_back([silu, plain], c, half)
 
-        def finish(c):
-            cols = slice(c * CHUNK, (c + 1) * CHUNK)
+        def finish(c, halves):
+            for half in halves:
+                result = ring.tile([P, PACK, CHUNK], F32, name="result", tag="result", bufs=3)
+                nc.vector.tensor_tensor(result[:], summed[(c, half)][:], a2[(half, c)], ALU.add)
+                store(c, half, result)
+
+        def last_products(c):
+            y1 = [psum.tile([P, BANK], F32, name="acc", tag="acc", bufs=4) for half in range(2)]
+            y2 = [psum.tile([P, PACK, CHUNK], F32, name="acc", tag="acc", bufs=4) for half in range(2)]
+            for half in range(2):
+                for a in range(2):
+                    product_w2(y1[half], c, a, half)
+            for half in range(2):
+                for a in range(2):
+                    x_codes, x_scales = x_q[(a, c)]
+                    codes, scales = w3_q[(a, half)]
+                    for t in range(PACK):
+                        nc.tensor.matmul_mx(
+                            out=y2[half][:, t, :],
+                            lhsT=codes[:, t * P : (t + 1) * P].bitcast(FP8X4),
+                            lhsT_scale=scales[:, t * P : (t + 1) * P],
+                            rhs=x_codes.bitcast(FP8X4),
+                            rhs_scale=x_scales,
+                            start=(a == 0 and t == 0),
+                            stop=(a == 1 and t == PACK - 1),
+                        )
+            turned = [turn_back([apply_silu(y1[half])], c, half) for half in range(2)]
+            partial = []
+            for half in range(2):
+                partial.append(ring.tile([P, PACK, CHUNK], F32, name="plain", tag="plain"))
+                nc.vector.tensor_tensor(partial[half][:], y2[half][:], a2[(half, c)], ALU.add)
             for half in range(2):
                 result = ring.tile([P, PACK, CHUNK], F32, name="result", tag="result", bufs=3)
-                nc.vector.tensor_tensor(result[:], summed[(c, half)][:], (a2_lo[:, c], a2_hi[c][:])[half], ALU.add)
-                nc.sync.dma_start(
-                    out=out[half * PASS : (half + 1) * PASS, cols].rearrange("(p t) j -> p t j", t=PACK),
-                    in_=result[:],
-                )
+                nc.vector.tensor_tensor(result[:], turned[half][:], partial[half][:], ALU.add)
+                store(c, half, result)
 
-        kept1 = ring.tile([P, PAIRS], F32, name="first", tag="first")
-        pick_kept(kept1, 1, 0)
-        pick_kept(kept0, 0, 3)
-        pick_kept(kept1, 1, 1)
+        kept1 = keep.tile([P, PACK * CHUNK], F32, name="kept1", tag="gate_a", align_bytes=64)
+        pick_kept(kept0, 1, 0, 3)
+        pick_kept(kept1, 1, 1, 0)
         max_first(3)
-        weave_scalar(0, xb_first, "after_x0")
-        pick_kept(kept1, 1, 2)
-        pick_kept(kept1, 1, 3)
-        nc.vector.tensor_tensor(
-            a2_hi[1][:], by_row(kept1[:, 0 : PACK * CHUNK]), third_lo[:, :, CHUNK : 2 * CHUNK], ALU.max
-        )
-        xb_second = ring.tile([P, PACK, CHUNK], BF16, name="xb", tag="xb")
+        weave_scalar(0, xb_first, "stage_b")
+        for t in range(1, PACK):
+            pick_kept(kept1, 1, 1, t)
+        w3_q[(0, 1)] = quantise(w3_grouped[(0, 1)][:], BANK, "w3q01", "kept0")
+        nc.vector.tensor_tensor(a2[(1, 1)], by_row(kept1[:]), third_lo[:, :, CHUNK : 2 * CHUNK], ALU.max)
+        xb_second = keep.tile([P, PACK, CHUNK], BF16, name="xb_second")
         for t in range(PACK):
             scale_rows(xb_second, 1, t)
-        weave_scalar(1, xb_second, "after_x1")
-        quantise_x(0)
+        weave_scalar(1, xb_second, "stage_a")
+        quantise_x(1, 0)
+        w3_q[(1, 1)] = quantise(w3_grouped[(1, 1)][:], BANK, "w3q11", "xb_first")
         products(0)
-        third_hi = keep.tile([P, PACK, KEPT // 2], F32, name="third_hi", tag="after_x0", align_bytes=64)
+        third_hi0 = keep.tile([P, PACK * HALF], F32, name="third_hi0", tag="stage_b", align_bytes=64)[:]
         for t in range(PACK):
-            nc.vector.tensor_copy(third_hi[:, t, :], hs[PACK + t][:].indirect(pos4_t[:, 16:32]))
-        quantise_x(1)
+            pick_third_hi(third_hi0, 0, t)
+        quantise_x(1, 1)
         products(1)
-        kept23 = keep.tile([P, 2, PACK * CHUNK], F32, name="kept23", tag="after_x1", align_bytes=64)
+        late = keep.tile([P, 2 * PACK * HALF], F32, name="late", tag="stage_a", align_bytes=64)
+        third_hi1 = late[:, 0 : PACK * HALF]
+        kept2 = [late[:, PACK * HALF + b * PACK * CHUNK : PACK * HALF + (b + 1) * PACK * CHUNK] for b in range(2)]
         for t in range(PACK):
-            pick_kept(kept23[:, 0, :], 2, t)
-        pick_kept(kept23[:, 1, :], 3, 0)
-        nc.vector.tensor_tensor(a2_hi[2][:], by_row(kept23[:, 0, :]), third_hi[:, :, 0:CHUNK], ALU.max)
-        pick_kept(kept23[:, 1, :], 3, 1)
-        weave_vector(2, "xg2")
-        pick_kept(kept23[:, 1, :], 3, 2)
-        quantise_x(2)
-        pick_kept(kept23[:, 1, :], 3, 3)
-        finish(0)
-        nc.vector.tensor_tensor(a2_hi[3][:], by_row(kept23[:, 1, :]), third_hi[:, :, CHUNK : 2 * CHUNK], ALU.max)
+            pick_kept(kept2[0], 0, 2, t)
+        pick_third_hi(third_hi1, 1, 0)
+        max_late(0, 2, kept2[0], third_hi0)
+        pick_third_hi(third_hi1, 1, 1)
+        weave_vector(0, 2, "xv02")
+        pick_third_hi(third_hi1, 1, 2)
+        for t in range(PACK):
+            pick_kept(kept2[1], 1, 2, t)
+        pick_third_hi(third_hi1, 1, 3)
+        quantise_x(0, 2)
+        max_late(1, 2, kept2[1], third_hi1)
+        pick_kept(kept2[0], 0, 3, 0)
+        weave_vector(1, 2, "xv12")
+        pick_kept(kept2[0], 0, 3, 1)
+        quantise_x(1, 2)
         products(2)
-        weave_vector(3, "a2_hi0")
-        finish(1)
-        quantise_x(3)
-        products(3)
-        finish(2)
-        finish(3)
+        pick_kept(kept2[0], 0, 3, 2)
+        pick_kept(kept2[0], 0, 3, 3)
+        finish(0, [1])
+        last = keep.tile([P, 2 * PACK * CHUNK], F32, name="last", tag="a2_10", align_bytes=64)
+        a2[(0, 3)] = by_row(last[:, 0 : PACK * CHUNK])
+        kept3 = last[:, PACK * CHUNK :]
+        for t in range(PACK):
+            pick_kept(kept3, 1, 3, t)
+        new_a2((1, 3), "a2_13")
+        max_late(0, 3, kept2[0], third_hi0)
+        max_late(1, 3, kept3, third_hi1)
+        weave_vector(0, 3, "xv03")
+        weave_vector(1, 3, "xv13")
+        quantise_x(0, 3)
+        quantise_x(1, 3)
+        finish(1, [1])
+        finish(2, [0, 1])
+        last_products(3)

from contextlib import ExitStack

import concourse.mybir as mybir
from concourse.masks import make_identity

K, H, T, S, PAIRS, KEPT = 512, 1024, 4096, 2048, 1024, 512
FLOPS = 2 * K * H * S + 2 * 2 * H * H * KEPT

F32 = mybir.dt.float32
BF16 = mybir.dt.bfloat16
I32 = mybir.dt.int32
U32 = mybir.dt.uint32
U16 = mybir.dt.uint16
U8 = mybir.dt.uint8
FP8X4 = mybir.dt.float8_e4m3fn_x4
FP4X4 = mybir.dt.float4_e2m1fn_x4
ACT = mybir.ActivationFunctionType
ALU = mybir.AluOpType

P = 128
PACK = 4
PASS = P * PACK
BANK = 512
CHUNK = 128
NCHUNK = KEPT // CHUNK


def tile_list_segment_triangulation_scores_kernel(
    tc, tab_words, tab_scales, offs, pos1, pos2, pos3, pos4, w1, gain, w2_words, w2_scales, w3, out
):
    nc = tc.nc
    with ExitStack() as ctx:
        keep = ctx.enter_context(tc.tile_pool(name="keep", bufs=1))
        ring = ctx.enter_context(tc.tile_pool(name="ring", bufs=2))
        psum = ctx.enter_context(tc.psum_pool(name="psum", bufs=1))

        offs_t = keep.tile([P, S // 16], U16, name="offs_t")
        pos1_t = keep.tile([P, PAIRS // 16], U16, name="pos1_t")
        pos2_t = keep.tile([P, PAIRS // 16], U16, name="pos2_t")
        pos3_t = keep.tile([P, KEPT // 16], U16, name="pos3_t")
        pos4_t = keep.tile([P, KEPT // 16], U16, name="pos4_t")

        tab_s = keep.tile([P, T], U8, name="tab_s", tag="stage_a", align_bytes=64)
        tab_w = keep.tile([P, T], U32, name="tab_w", tag="stage_c", align_bytes=64)
        gain_t = keep.tile([P, 2, PACK], F32, name="gain_t")
        ident = keep.tile([P, P], F32, name="ident")

        nc.sync.dma_start(out=tab_s[P - 16 :, :].bitcast(I32), in_=tab_scales[0].bitcast(I32))
        nc.sync.dma_start(offs_t[:], offs)
        nc.vector.memset(tab_s[0 : P - 16, :].bitcast(I32), 0)
        make_identity(nc, ident[:])
        warm = keep.tile([P, 1], F32, name="warm")
        nc.scalar.activation(out=warm[:], in_=ident[:, 0:1], func=ACT.Silu)

        def load_raw(w, a, c0, width, tag):
            raw = keep.tile([P, PACK, width], F32, name="raw", tag=tag, align_bytes=64)
            nc.sync.dma_start(
                out=raw[:],
                in_=w[a * PASS : (a + 1) * PASS, c0 : c0 + width].rearrange("(p j) c -> p j c", j=PACK),
            )
            return raw

        def quantise(grouped, width, name, tag=None):
            codes = keep.tile([P, width], U32, name=name + "_c", tag=tag or name + "_c", align_bytes=64)
            scales = keep.tile([P, width], U8, name=name + "_s", align_bytes=64)
            nc.vector.quantize_mx(out=codes[:].bitcast(FP8X4), scales=scales[:], in_=grouped)
            return codes, scales

        def prepare_w1(raws, b, t0):
            grouped = ring.tile([P, PACK * BANK], BF16, name="grouped", tag="grouped", align_bytes=64)
            dst = grouped[:].rearrange("p (t m j) -> p m j t", t=PACK, j=PACK)
            for i, raw in enumerate(raws):
                src = raw.rearrange("p j (m t) -> p m j t", t=PACK)
                nc.scalar.copy(out=dst[:, i * P // 2 : (i + 1) * P // 2, :, t0:], in_=src[:, :, :, t0:])
            codes, scales = quantise(grouped[:, t0 * BANK :], (PACK - t0) * P, "w1q%d" % b)
            for t in range(t0, PACK):
                cols = slice((t - t0) * P, (t - t0 + 1) * P)
                w1_q[PACK * b + t] = (codes[:, cols], scales[:, cols])

        def round_w3(raw, last):
            if last:
                grouped = keep.tile([P, PACK * BANK], BF16, name="grouped", tag="gate_b", align_bytes=64)
            else:
                grouped = ring.tile([P, PACK * BANK], BF16, name="grouped", tag="grouped", align_bytes=64)
            nc.scalar.copy(
                out=grouped[:].rearrange("p (t m j) -> p m j t", t=PACK, j=PACK),
                in_=raw[:].rearrange("p j (m t) -> p m j t", t=PACK),
            )
            return grouped

        nc.sync.dma_start(
            out=tab_w[:].bitcast(I32), in_=tab_words[0].rearrange("p t i -> p (t i)").bitcast(I32)
        )
        nc.sync.dma_start(pos1_t[:], pos1)
        nc.sync.dma_start(pos2_t[:], pos2)
        nc.sync.dma_start(out=gain_t[:], in_=gain.rearrange("(b p t) -> p b t", b=2, t=PACK))
        w1_raw0 = [load_raw(w1, 0, 0, BANK // 2, "stage_b")[:], load_raw(w1, 0, BANK // 2, BANK // 2, "stage_e")[:]]
        nc.sync.dma_start(pos4_t[:], pos4)
        nc.sync.dma_start(pos3_t[:], pos3)

        v_rows = keep.tile([P, S], U8, name="v_rows", tag="stage_d", align_bytes=64)
        v_s = keep.tile([P, S], U8, name="v_s", align_bytes=64)
        nc.vector.memset(v_s[:].bitcast(I32), 0)
        nc.vector.tensor_copy(v_rows[:], tab_s[:].indirect(offs_t[:]))
        for q in range(4):
            nc.sync.dma_start(
                out=v_s[32 * q : 32 * q + 4, :].bitcast(I32),
                in_=v_rows[P - 16 + 4 * q : P - 12 + 4 * q, :].bitcast(I32),
            )
        w1_second = load_raw(w1, 0, BANK, BANK, "stage_a")
        w1_raw1 = [w1_second[:, :, 0 : BANK // 2], w1_second[:, :, BANK // 2 :]]
        lead = keep.tile([P, PACK * P], BF16, name="lead", tag="v_w3", align_bytes=64)
        for i, raw in enumerate(w1_raw0):
            nc.scalar.copy(
                out=lead[:].rearrange("p (m j) -> p m j", j=PACK)[:, i * P // 2 : (i + 1) * P // 2],
                in_=raw.rearrange("p j (m t) -> p t m j", t=PACK)[:, 0],
            )
        w1_q = {0: quantise(lead[:], P, "w1lead")}
        v_w = []
        for q in range(S // BANK):
            piece = keep.tile([P, BANK], U32, name="v_w%d" % q, tag="v_w%d" % q, align_bytes=64)
            nc.vector.tensor_copy(piece[:], tab_w[:].indirect(offs_t[:, 32 * q : 32 * q + 32]))
            v_w.append(piece)

        def features(s):
            codes, scales = w1_q[s]
            if s < 2 * PACK - 1:
                h = ring.tile([P, S], F32, name="h", tag="h", bufs=2 * PACK - 1)
            else:
                h = keep.tile([P, S], F32, name="h", tag="stage_c", align_bytes=64)
            for q in range(S // BANK):
                if s < 2 * PACK - 1:
                    acc = psum.tile([P, BANK], F32, name="acc", tag="acc", bufs=4)
                else:
                    acc = psum.tile([P, BANK], F32, name="acc", tag="turned%d" % q)
                nc.tensor.matmul_mx(
                    out=acc[:],
                    lhsT=codes[:].bitcast(FP8X4),
                    lhsT_scale=scales[:],
                    rhs=v_w[q][:].bitcast(FP8X4),
                    rhs_scale=v_s[:, q * BANK : (q + 1) * BANK],
                    start=True,
                    stop=True,
                )
                nc.scalar.activation(out=h[:, q * BANK : (q + 1) * BANK], in_=acc[:], func=ACT.Tanh)
            return h

        hs = [features(0)]
        prepare_w1(w1_raw0, 0, 1)
        hs.extend(features(s) for s in range(1, 3))
        prepare_w1(w1_raw1, 1, 0)
        hs.extend(features(s) for s in range(3, 2 * PACK))

        w2_s = keep.tile([P, 2, H], U8, name="w2_s", tag="stage_e", align_bytes=64)
        w2_w = keep.tile([P, 2, 2 * H], U8, name="w2_w", tag="stage_d", align_bytes=64)
        nc.vector.memset(w2_s[:].rearrange("p a c -> p (a c)").bitcast(I32), 0)
        nc.sync.dma_start(
            out=w2_w[:].bitcast(I32), in_=w2_words.rearrange("a p c -> p a c").bitcast(I32)
        )
        for q in range(4):
            nc.sync.dma_start(
                out=w2_s[32 * q : 32 * q + 4].bitcast(I32),
                in_=w2_scales[:, 4 * q : 4 * q + 4, :].rearrange("a r c -> r a c").bitcast(I32),
            )
        w3_q = {}

        w3_grouped = {}
        for half in range(2):
            for a in range(2):
                raw = load_raw(w3, a, half * BANK, BANK, ("stage_b", "stage_a")[a])
                w3_grouped[(a, half)] = round_w3(raw, (a, half) == (1, 0))
                if half == 0:
                    w3_q[(a, half)] = quantise(w3_grouped[(a, half)][:], BANK, "w3q%d0" % a)

        HALF = KEPT // 2
        a2_early = keep.tile([P, 2, PACK, CHUNK], F32, name="a2_early", tag="a2_early", align_bytes=64)
        a2 = {(0, 0): a2_early[:, 0], (0, 1): a2_early[:, 1]}

        def new_a2(key, tag):
            a2[key] = keep.tile([P, PACK, CHUNK], F32, name="a2_%d%d" % key, tag=tag, align_bytes=64)[:]

        for key in ((0, 2), (1, 0), (1, 1), (1, 2)):
            new_a2(key, "a2_%d%d" % key)
        third_lo = keep.tile([P, PACK, HALF], F32, name="third_lo")
        kept0 = keep.tile([P, PACK * CHUNK], F32, name="kept0", tag="kept0", align_bytes=64)
        xb_first = keep.tile([P, PACK, CHUNK], BF16, name="xb_first", tag="xb_first", align_bytes=64)
        a1 = []
        picked = {}
        x_q = {}
        xg = {}

        def pick_kept(dst, b, c, t):
            nc.vector.tensor_copy(
                dst[:, t * CHUNK : (t + 1) * CHUNK], a1[PACK * b + t][:].indirect(pos3_t[:, 8 * c : 8 * c + 8])
            )

        def pick_third_hi(dst, b, t):
            nc.vector.tensor_copy(dst[:, t * HALF : (t + 1) * HALF], hs[PACK * b + t][:].indirect(pos4_t[:, 16:32]))

        def scale_rows(xb, c, t):
            nc.scalar.activation(
                out=xb[:, t, :], in_=a2[(1, c)][:, t, :], func=ACT.Copy, scale=gain_t[:, 1, t : t + 1]
            )

        def max_first(t):
            nc.vector.tensor_tensor(
                a2[(1, 0)][:, t, :], kept0[:, t * CHUNK : (t + 1) * CHUNK], third_lo[:, t, 0:CHUNK], ALU.max
            )
            scale_rows(xb_first, 0, t)

        a2_turned = {}

        def turn_residual(b, c):
            bank = psum.tile([P, PACK, P], F32, name="turned", tag="turned%d" % (2 + c))
            for t in range(PACK):
                nc.tensor.transpose(bank[:, t, :], a2[(b, c)][:, t, :], ident[:])
            a2_turned[(b, c)] = keep.tile([P, PACK, P], F32, name="a2_turned%d%d" % (b, c))
            nc.scalar.copy(out=a2_turned[(b, c)][:], in_=bank[:])

        for s in range(2 * PACK):
            b, t = divmod(s, PACK)
            h = hs[s]
            if s < 2 * PACK - 2:
                first = ring.tile([P, PAIRS], F32, name="first", tag="first")
            else:
                first = keep.tile([P, PAIRS], F32, name="first", tag=("gate_b", "gate_a")[s % 2], align_bytes=64)
            nc.vector.tensor_copy(first[:], h[:].indirect(pos1_t[:]))
            if 1 <= s <= PACK:
                kept = ring.tile([P, HALF], F32, name="kept", tag="kept")
                nc.vector.tensor_copy(kept[:], a1[s - 1][:].indirect(pos3_t[:, 0:16]))
            elif s > PACK:
                pick_kept(kept0, 1, 0, t - 1)
            if b == 0:
                third = ring.tile([P, HALF], F32, name="third", tag="third")
                nc.vector.tensor_copy(third[:], h[:].indirect(pos4_t[:, 0:16]))
                picked[s] = third
            else:
                nc.vector.tensor_copy(third_lo[:, t, :], h[:].indirect(pos4_t[:, 0:16]))
            pair = ring.tile([P, PAIRS], F32, name="pair", tag="pair", bufs=2 * PACK)
            nc.vector.tensor_tensor(pair[:], h[:].indirect(pos2_t[:]), first[:], ALU.mult)
            a1.append(pair)
            if 1 <= s <= PACK:
                nc.vector.tensor_tensor(
                    a2_early[:, :, s - 1, :],
                    kept[:].rearrange("p (c j) -> p c j", c=2),
                    picked[s - 1][:].rearrange("p (c j) -> p c j", c=2),
                    ALU.max,
                )
            elif s > PACK:
                max_first(t - 1)
            if s == PACK:
                xb0 = keep.tile([P, PACK, HALF], BF16, name="xb0")
                for tt in range(PACK):
                    nc.scalar.activation(
                        out=xb0[:, tt, :].rearrange("p (c j) -> p c j", c=2),
                        in_=a2_early[:, :, tt, :],
                        func=ACT.Copy,
                        scale=gain_t[:, 0, tt : tt + 1],
                    )
                xg0 = keep.tile([P, PACK * HALF], BF16, name="xg0", tag="gate_a", align_bytes=64)
                nc.scalar.copy(
                    out=xg0[:].rearrange("p (c i t) -> p c t i", i=4, t=PACK),
                    in_=xb0[:].rearrange("p t (c i) -> p c t i", i=4),
                )
                turn_residual(0, 0)
                turn_residual(0, 1)
            if s == PACK + 1:
                codes, scales = quantise(xg0[:], HALF, "xq_early")
                for c in range(2):
                    cols = slice(c * CHUNK, (c + 1) * CHUNK)
                    x_q[(0, c)] = (codes[:, cols], scales[:, cols])

        def by_row(ap):
            return ap.rearrange("p (t j) -> p t j", t=PACK)

        def weave_scalar(c, xb, tag):
            xg[(1, c)] = keep.tile([P, PACK * CHUNK], BF16, name="xg%d" % c, tag=tag, align_bytes=64)
            nc.scalar.copy(
                out=xg[(1, c)][:].rearrange("p (c i t) -> p c t i", i=4, t=PACK),
                in_=xb[:].rearrange("p t (c i) -> p c t i", i=4),
            )

        def weave_vector(b, c, tag):
            xg[(b, c)] = keep.tile([P, PACK * CHUNK], BF16, name="xv%d%d" % (b, c), tag=tag, align_bytes=64)
            nc.vector.tensor_tensor(
                xg[(b, c)][:].rearrange("p (c i t) -> p c t i", i=4, t=PACK),
                a2[(b, c)].rearrange("p t (c i) -> p c t i", i=4),
                gain_t[:, b : b + 1, :].unsqueeze(3).to_broadcast([P, CHUNK // 4, PACK, 4]),
                ALU.mult,
            )

        def quantise_x(b, c):
            codes, scales = quantise(xg[(b, c)][:], CHUNK, "xq%d%d" % (b, c))
            x_q[(b, c)] = (codes[:], scales[:])

        def max_late(b, c, kept, third_hi):
            nc.vector.tensor_tensor(
                a2[(b, c)], by_row(kept), by_row(third_hi)[:, :, (c - 2) * CHUNK : (c - 1) * CHUNK], ALU.max
            )

        summed = {}

        def turned_product(bank, c, a, half, rhs, rhs_scale):
            codes, scales = x_q[(a, c)]
            nc.tensor.matmul_mx(
                out=bank[:],
                lhsT=codes.bitcast(FP8X4),
                lhsT_scale=scales,
                rhs=rhs,
                rhs_scale=rhs_scale,
                start=(a == 0),
                stop=(a == 1),
            )

        def product_w2(bank, c, a, half):
            turned_product(
                bank,
                c,
                a,
                half,
                w2_w[:, a, 2 * BANK * half : 2 * BANK * (half + 1)].bitcast(FP4X4),
                w2_s[:, a, BANK * half : BANK * (half + 1)],
            )

        def apply_silu(y1):
            silu = ring.tile([P, PACK, P], F32, name="silu", tag="silu")
            nc.scalar.activation(out=silu[:], in_=y1[:].rearrange("p (m t) -> p t m", t=PACK), func=ACT.Silu)
            return silu

        def turn_back(terms, c, half):
            bank = ((0, 1), (2, 3), (0, 2), (1, 3))[c][half]
            turned = psum.tile([P, PACK, CHUNK], F32, name="turned", tag="turned%d" % bank)
            for t in range(PACK):
                for i, term in enumerate(terms):
                    nc.tensor.matmul(
                        turned[:, t, :],
                        term[:, t, :],
                        ident[:],
                        start=(i == 0),
                        stop=(i == len(terms) - 1),
                        is_transpose=True,
                    )
            return turned

        def store(c, half, result):
            nc.sync.dma_start(
                out=out[half * PASS : (half + 1) * PASS, c * CHUNK : (c + 1) * CHUNK].rearrange(
                    "(p t) j -> p t j", t=PACK
                ),
                in_=result[:],
            )

        def products(c):
            for half in range(2):
                y1 = psum.tile([P, BANK], F32, name="acc", tag="acc", bufs=4)
                y2 = psum.tile([P, BANK], F32, name="acc", tag="acc", bufs=4)
                for a in range(2):
                    product_w2(y1, c, a, half)
                    turned_product(y2, c, a, half, w3_q[(a, half)][0][:].bitcast(FP8X4), w3_q[(a, half)][1][:])
                silu = apply_silu(y1)
                plain = ring.tile([P, PACK, P], F32, name="plain", tag="plain")
                nc.scalar.copy(out=plain[:], in_=y2[:].rearrange("p (t m) -> p t m", t=PACK))
                if (half, c) in a2_turned:
                    turned = turn_back([silu, plain, a2_turned[(half, c)]], c, half)
                    result = ring.tile([P, PACK, CHUNK], F32, name="result", tag="result", bufs=3)
                    nc.scalar.copy(out=result[:], in_=turned[:])
                    store(c, half, result)
                else:
                    summed[(c, half)] = turn_back([silu, plain], c, half)

        def finish(c, halves):
            for half in halves:
                result = ring.tile([P, PACK, CHUNK], F32, name="result", tag="result", bufs=3)
                nc.vector.tensor_tensor(result[:], summed[(c, half)][:], a2[(half, c)], ALU.add)
                store(c, half, result)

        def last_products(c):
            y1 = [psum.tile([P, BANK], F32, name="acc", tag="acc", bufs=4) for half in range(2)]
            y2 = [psum.tile([P, PACK, CHUNK], F32, name="acc", tag="acc", bufs=4) for half in range(2)]
            for half in range(2):
                for a in range(2):
                    product_w2(y1[half], c, a, half)
            for half in range(2):
                for a in range(2):
                    x_codes, x_scales = x_q[(a, c)]
                    codes, scales = w3_q[(a, half)]
                    for t in range(PACK):
                        nc.tensor.matmul_mx(
                            out=y2[half][:, t, :],
                            lhsT=codes[:, t * P : (t + 1) * P].bitcast(FP8X4),
                            lhsT_scale=scales[:, t * P : (t + 1) * P],
                            rhs=x_codes.bitcast(FP8X4),
                            rhs_scale=x_scales,
                            start=(a == 0 and t == 0),
                            stop=(a == 1 and t == PACK - 1),
                        )
            turned = [turn_back([apply_silu(y1[half])], c, half) for half in range(2)]
            partial = []
            for half in range(2):
                partial.append(ring.tile([P, PACK, CHUNK], F32, name="plain", tag="plain"))
                nc.vector.tensor_tensor(partial[half][:], y2[half][:], a2[(half, c)], ALU.add)
            for half in range(2):
                result = ring.tile([P, PACK, CHUNK], F32, name="result", tag="result", bufs=3)
                nc.vector.tensor_tensor(result[:], turned[half][:], partial[half][:], ALU.add)
                store(c, half, result)

        kept1 = keep.tile([P, PACK * CHUNK], F32, name="kept1", tag="gate_a", align_bytes=64)
        pick_kept(kept0, 1, 0, 3)
        pick_kept(kept1, 1, 1, 0)
        max_first(3)
        weave_scalar(0, xb_first, "stage_b")
        for t in range(1, PACK):
            pick_kept(kept1, 1, 1, t)
        w3_q[(0, 1)] = quantise(w3_grouped[(0, 1)][:], BANK, "w3q01", "kept0")
        nc.vector.tensor_tensor(a2[(1, 1)], by_row(kept1[:]), third_lo[:, :, CHUNK : 2 * CHUNK], ALU.max)
        xb_second = keep.tile([P, PACK, CHUNK], BF16, name="xb_second")
        for t in range(PACK):
            scale_rows(xb_second, 1, t)
        weave_scalar(1, xb_second, "stage_a")
        quantise_x(1, 0)
        w3_q[(1, 1)] = quantise(w3_grouped[(1, 1)][:], BANK, "w3q11", "xb_first")
        products(0)
        third_hi0 = keep.tile([P, PACK * HALF], F32, name="third_hi0", tag="stage_b", align_bytes=64)[:]
        for t in range(PACK):
            pick_third_hi(third_hi0, 0, t)
        quantise_x(1, 1)
        products(1)
        late = keep.tile([P, 2 * PACK * HALF], F32, name="late", tag="stage_a", align_bytes=64)
        third_hi1 = late[:, 0 : PACK * HALF]
        kept2 = [late[:, PACK * HALF + b * PACK * CHUNK : PACK * HALF + (b + 1) * PACK * CHUNK] for b in range(2)]
        for t in range(PACK):
            pick_kept(kept2[0], 0, 2, t)
        pick_third_hi(third_hi1, 1, 0)
        max_late(0, 2, kept2[0], third_hi0)
        pick_third_hi(third_hi1, 1, 1)
        weave_vector(0, 2, "xv02")
        pick_third_hi(third_hi1, 1, 2)
        for t in range(PACK):
            pick_kept(kept2[1], 1, 2, t)
        pick_third_hi(third_hi1, 1, 3)
        quantise_x(0, 2)
        max_late(1, 2, kept2[1], third_hi1)
        pick_kept(kept2[0], 0, 3, 0)
        weave_vector(1, 2, "xv12")
        pick_kept(kept2[0], 0, 3, 1)
        quantise_x(1, 2)
        products(2)
        pick_kept(kept2[0], 0, 3, 2)
        pick_kept(kept2[0], 0, 3, 3)
        finish(0, [1])
        last = keep.tile([P, 2 * PACK * CHUNK], F32, name="last", tag="a2_10", align_bytes=64)
        a2[(0, 3)] = by_row(last[:, 0 : PACK * CHUNK])
        kept3 = last[:, PACK * CHUNK :]
        for t in range(PACK):
            pick_kept(kept3, 1, 3, t)
        new_a2((1, 3), "a2_13")
        max_late(0, 3, kept2[0], third_hi0)
        max_late(1, 3, kept3, third_hi1)
        weave_vector(0, 3, "xv03")
        weave_vector(1, 3, "xv13")
        quantise_x(0, 3)
        quantise_x(1, 3)
        finish(1, [1])
        finish(2, [0, 1])
        last_products(3)
